import numpy as np
import ml_dtypes


def mxq(x, axis, fmt="e4m3"):
    dtype, down = {"e4m3": (ml_dtypes.float8_e4m3fn, 7), "e5m2": (ml_dtypes.float8_e5m2, 14)}[fmt]
    v = np.moveaxis(np.asarray(x, np.float32).astype(ml_dtypes.bfloat16).astype(np.float64), axis, -1)
    blocks = v.reshape(v.shape[:-1] + (-1, 32))
    amax = np.abs(blocks).max(-1, keepdims=True)
    byte = np.maximum(np.where(amax > 0, np.frexp(amax)[1] - 1 + 127, 0) - down, 1)
    scale = np.exp2(byte - 127.0)
    codes = (blocks / scale).astype(np.float32).astype(dtype).astype(np.float64)
    return np.moveaxis((codes * scale).reshape(v.shape), -1, axis)


WIDE = False


def mx_kscale(k):
    if not WIDE:
        return np.ones(k)
    levels = np.array([10, -10, 5, -5, 0])
    if k % 512:
        return np.exp2(np.random.permutation(np.resize(levels, k // 32))).repeat(32)
    a = np.empty((k // 512, 16))
    for p in range(k // 512):
        a[p, :8] = np.random.permutation(np.resize(levels, 8))
        for g in range(8):
            far = levels[np.abs(levels - a[p, g]) >= 10]
            a[p, g + 8] = far[np.random.randint(len(far))]
    return np.exp2(a.ravel()).repeat(32)


def f64(x):
    return np.asarray(x).astype(np.float64)


def striped(idx):
    return np.tile(idx.reshape(-1, 16).T, (8, 1)).astype(np.uint16)


def unstriped(offs):
    return offs[:16].T.reshape(-1).astype(np.int64)


def striped8(idx):
    return np.concatenate([x.reshape(-1, 16).T for x in idx]).astype(np.uint16)


def runs(offs, k):
    lists = np.stack([offs[16 * r : 16 * r + 16].T.reshape(-1) for r in range(8)]).astype(np.int64)
    return lists[np.arange(k) % 512 // 64]


def pack_weight(w):
    k, n = w.shape
    w = f64(np.asarray(w, np.float32).astype(ml_dtypes.bfloat16)).reshape(k // 32, 32, n)
    amax = np.abs(w).max(1)
    byte = np.clip(np.where(amax > 0, np.frexp(amax)[1] - 1 + 127 - 7, 1), 1, 254)
    scaled = (w * np.exp2(127.0 - byte)[:, None, :]).reshape(k, n).astype(np.float32)
    words = np.ascontiguousarray(scaled.reshape(k // 512, 128, 4, n).transpose(0, 1, 3, 2)).astype(ml_dtypes.float8_e4m3fn).view(np.uint8)
    return words, np.ascontiguousarray(byte.astype(np.uint8).reshape(k // 512, 16, n))


def unpack_weight(words, scales):
    g, p, n, _ = words.shape
    vals = np.ascontiguousarray(words).view(ml_dtypes.float8_e4m3fn).astype(np.float64) * np.repeat(np.exp2(scales.astype(np.float64) - 127.0), 8, axis=1)[..., None]
    return vals.transpose(0, 1, 3, 2).reshape(g * 512, n)


K, T, S, N, G, H = 512, 1024, 256, 512, 2048, 512


def setup_inputs():
    n = np.random.standard_normal
    s = mx_kscale(K)[:, None]
    u = mx_kscale(K)
    packed_xT = pack_weight(n((K, T)) * s)
    packed_dT = pack_weight(n((K, G)) / s)
    return {
        "x_words": packed_xT[0],
        "x_scales": packed_xT[1],
        "d_words": packed_dT[0],
        "d_scales": packed_dT[1],
        "gn": (np.random.uniform(0.5, 1.5, (H, 1)) * u[:, None]).astype(np.float32),
        "w1": (n((H, N)) / np.sqrt(H) / u[:, None]).astype(np.float32),
        "offs": striped(np.random.permutation(T)[:S]),
        "k1": striped8(np.random.randint(0, G, (8, H))),
        "two": striped(np.random.permutation(T)[:S]),
        "k2": striped8(np.random.randint(0, G, (8, H))),
        "n1": striped8(np.stack([np.random.permutation(S) for _ in range(8)])),
        "n2": striped8(np.stack([np.random.permutation(S) for _ in range(8)])),
        "n3": striped8(np.stack([np.random.permutation(S) for _ in range(8)])),
        "n4": striped8(np.stack([np.random.permutation(S) for _ in range(8)])),
        "n5": striped8(np.stack([np.random.permutation(S) for _ in range(8)])),
        "n6": striped8(np.stack([np.random.permutation(S) for _ in range(8)])),
    }


def reference(x_words, x_scales, d_words, d_scales, gn, w1, offs, k1, two, k2, n1, n2, n3, n4, n5, n6):
    d_k1 = unpack_weight(d_words, d_scales)[np.arange(K)[:, None], runs(k1, K)]
    xq = unpack_weight(x_words, x_scales)[:, unstriped(offs)]
    a = 0.0625 * (d_k1.T @ xq)
    d_k2 = unpack_weight(d_words, d_scales)[np.arange(K)[:, None], runs(k2, K)]
    x_two = unpack_weight(x_words, x_scales)[:, unstriped(two)]
    b = 0.0625 * (d_k2.T @ x_two)
    z = f64(gn) * (a * (np.tanh(b[np.arange(H)[:, None], runs(n1, H)] - (b[np.arange(H)[:, None], runs(n2, H)]))))
    h = mxq(f64(w1), 0, "e4m3").T @ mxq(z, 0, "e4m3")
    return 0.75 * ((h[np.arange(N)[:, None], runs(n3, N)]) * (h[np.arange(N)[:, None], runs(n4, N)]) - ((h[np.arange(N)[:, None], runs(n5, N)]) * (h[np.arange(N)[:, None], runs(n6, N)])))

@@ -1,0 +1,236 @@
+from contextlib import ExitStack
+
+import concourse.mybir as mybir
+
+K, T, S, N, G, H = 512, 1024, 256, 512, 2048, 512
+FLOPS = 3 * 2 * 512 * 512 * 256
+
+F32 = mybir.dt.float32
+BF16 = mybir.dt.bfloat16
+I32 = mybir.dt.int32
+U32 = mybir.dt.uint32
+U16 = mybir.dt.uint16
+U8 = mybir.dt.uint8
+FP8X4 = mybir.dt.float8_e4m3fn_x4
+ACT = mybir.ActivationFunctionType
+ALU = mybir.AluOpType
+
+P = 128
+SLOTS = 4
+RUN = 8
+WINDOW = 2 * S
+HALF = S // 2
+
+
+def tile_picked_twpqjointbdet_none_p_kernel(
+    tc, x_words, x_scales, d_words, d_scales, gn, w1, offs, k1, two, k2, n1, n2, n3, n4, n5, n6, out
+):
+    nc = tc.nc
+    with ExitStack() as ctx:
+        sb = ctx.enter_context(tc.tile_pool(name="sb", bufs=1))
+        ps = ctx.enter_context(tc.psum_pool(name="ps", bufs=1))
+
+        def load_list(name, src):
+            tile = sb.tile([P, src.shape[1]], U16, name=name)
+            nc.sync.dma_start(tile[:], src)
+            return tile
+
+        def load_scales(name, src):
+            width = src.shape[2]
+            tile = sb.tile([P, width], U8, name=name, align_bytes=64)
+            rows = src[0].bitcast(I32).unsqueeze(1).to_broadcast([16, RUN, width // 4])
+            nc.scalar.dma_start(tile[:].bitcast(I32), rows)
+            return tile
+
+        def load_words(name, src, queue):
+            tile = sb.tile([P, src.shape[2]], I32, name=name, align_bytes=64)
+            queue.dma_start(tile[:], src[0].rearrange("p n t -> p (n t)").bitcast(I32))
+            return tile
+
+        ds_win = load_scales("ds_win", d_scales)
+        k2_t = load_list("k2_t", k2)
+        xs_win = load_scales("xs_win", x_scales)
+        two_t = load_list("two_t", two)
+        dw_win = load_words("dw_win", d_words, nc.scalar)
+        k1_t = load_list("k1_t", k1)
+        offs_t = load_list("offs_t", offs)
+        n1_t = load_list("n1_t", n1)
+        n2_t = load_list("n2_t", n2)
+        n5_t = load_list("n5_t", n5)
+        xw_win = load_words("xw_win", x_words, nc.sync)
+        n6_t = load_list("n6_t", n6)
+        n3_t = load_list("n3_t", n3)
+        n4_t = load_list("n4_t", n4)
+
+        planes = {}
+        for name in ("b", "a"):
+            planes[name] = sb.tile([P, H + S], U8, name=name + "_plane", align_bytes=64)
+            nc.gpsimd.memset(planes[name][:].bitcast(I32), 0)
+        wins = [sb.tile([P, WINDOW], F32, name=f"win{t}", align_bytes=64) for t in range(SLOTS)]
+        for t in range(SLOTS):
+            nc.gpsimd.memset(wins[t][:, S:], 0.0)
+
+        gn_raw = sb.tile([P, 8 * SLOTS], F32, name="gn_raw")
+        gn_rows = gn.rearrange("(g t u) o -> t g u o", t=SLOTS, u=RUN)
+        with nc.allow_non_contiguous_dma(reason="one gain for each partition and slot"):
+            for t in range(SLOTS):
+                nc.gpsimd.dma_start(gn_raw[:, 8 * t : 8 * t + 1], gn_rows[t])
+        gn16 = sb.tile([P, SLOTS], F32, name="gn16")
+        nc.gpsimd.tensor_scalar(gn16[:], gn_raw[:, ::8], 0.0625, 0.0, ALU.mult, ALU.add)
+
+        def deal(dst, src, run):
+            nc.vector.tensor_copy(
+                dst.rearrange("p (t g u) -> p t g u", t=SLOTS, u=run),
+                src.rearrange("p (g t u) -> p t g u", t=SLOTS, u=run),
+            )
+
+        def product(bank, t, lhs, lhs_scale, rhs, rhs_scale):
+            cols = slice(t * P, (t + 1) * P)
+            nc.tensor.matmul_mx(
+                out=bank,
+                lhsT=lhs[:, cols].bitcast(FP8X4),
+                lhsT_scale=lhs_scale[:, cols],
+                rhs=rhs.bitcast(FP8X4),
+                rhs_scale=rhs_scale,
+                start=True,
+                stop=True,
+            )
+
+        def token_words(name, token_list):
+            x_codes = sb.tile([P, S], U32, name=name + "_xc", align_bytes=64)
+            nc.vector.tensor_copy(x_codes[:], xw_win[:].bitcast(U32).indirect(token_list[:]))
+            return x_codes
+
+        def scale_plane(name, dict_list, token_list, queue, tag):
+            got = sb.tile([P, H + S], U8, name=name + "_bytes", tag=tag, align_bytes=64)
+            stage = sb.tile([P, H + S], U8, name=name + "_stage", align_bytes=64)
+            nc.vector.tensor_copy(got[:, :H], ds_win[:].indirect(dict_list[:]))
+            nc.vector.tensor_copy(got[:, H:], xs_win[:].indirect(token_list[:]))
+            deal(stage[:, :H].bitcast(I32), got[:, :H].bitcast(I32), RUN // 4)
+            nc.vector.tensor_copy(stage[:, H:].bitcast(I32), got[:, H:].bitcast(I32))
+            for r in range(4):
+                queue.dma_start(planes[name][r:P:32, :].bitcast(I32), stage[RUN * r : P : 32, :].bitcast(I32))
+
+        def dict_words(name, dict_list, tag):
+            d_got = sb.tile([P, H], U32, name=name + "_dg", tag=tag, align_bytes=64)
+            nc.vector.tensor_copy(d_got[:], dw_win[:].bitcast(U32).indirect(dict_list[:]))
+            return d_got
+
+        def dealt_words(name, d_got):
+            d_codes = sb.tile([P, H], U32, name=name + "_dc", align_bytes=64)
+            deal(d_codes[:].bitcast(I32), d_got[:].bitcast(I32), RUN)
+            return d_codes
+
+        scale_plane("b", k2_t, two_t, nc.scalar, "b_xb")
+        b_got = dict_words("b", k2_t, "b_dg")
+        b_x = token_words("b", two_t)
+        b_d = dealt_words("b", b_got)
+        a_x = token_words("a", offs_t)
+        b_banks = [ps.tile([P, S], F32, name=f"bh{t}") for t in range(SLOTS)]
+        for t in range(SLOTS):
+            product(b_banks[t][:], t, b_d, planes["b"], b_x[:], planes["b"][:, H:])
+
+        w_raw = sb.tile([P, SLOTS, N], F32, name="w_raw", tag="b_xb", align_bytes=64)
+        w_rows = w1.rearrange("(g t u) m -> t g u m", t=SLOTS, u=RUN)
+        for t in range(SLOTS):
+            nc.sync.dma_start(w_raw[:, t, :], w_rows[t])
+
+        scale_plane("a", k1_t, offs_t, nc.sync, "xw_win")
+        a_d = dealt_words("a", dict_words("a", k1_t, "b_xc"))
+        a_pairs = [ps.tile([P, 2, S], F32, name=f"a{pair}") for pair in range(2)]
+        a_rows = [a_pairs[t // 2][:, t % 2, :] for t in range(SLOTS)]
+        for t in range(SLOTS):
+            product(a_rows[t], t, a_d, planes["a"], a_x[:], planes["a"][:, H:])
+
+        def fetch(dst, t, lst, cols):
+            nc.scalar.activation(dst[:, cols], wins[t][:].indirect(lst[:, cols.start // 16 : cols.stop // 16]), ACT.Copy)
+
+        def rows_tile(name, tag=None):
+            return sb.tile([P, S], F32, name=name, tag=tag or name, align_bytes=64)
+
+        whole = slice(0, S)
+        halves = [slice(0, HALF), slice(HALF, S)]
+        last = SLOTS - 1
+
+        w_bf = sb.tile([P, N * SLOTS], BF16, name="w_bf", align_bytes=64)
+        w_codes = sb.tile([P, N], U32, name="w_codes", align_bytes=64)
+        w_plane = sb.tile([P, N], U8, name="w_plane", align_bytes=64)
+        z_rows = sb.tile([P, SLOTS, S], BF16, name="z_rows", align_bytes=64)
+        first = [rows_tile(f"first{t}") for t in range(SLOTS)]
+        second = [rows_tile(f"second{t}") for t in range(SLOTS)]
+        diff = {}
+        gate = [rows_tile(f"gate{t}") for t in range(SLOTS)]
+
+        def subtract(t, cols):
+            nc.vector.tensor_tensor(diff[t][:, cols], first[t][:, cols], second[t][:, cols], ALU.subtract)
+
+        def gated(t, cols):
+            nc.scalar.activation(gate[t][:, cols], diff[t][:, cols], ACT.Tanh, scale=0.0625)
+            nc.vector.scalar_tensor_tensor(
+                z_rows[:, t, cols], a_rows[t][:, cols], gn16[:, t : t + 1], gate[t][:, cols], ALU.mult, ALU.mult
+            )
+
+        def difference(t, tag=None):
+            nc.scalar.copy(wins[t][:, :S], b_banks[t][:])
+            fetch(first[t], t, n1_t, whole)
+            fetch(second[t], t, n2_t, whole)
+            diff[t] = rows_tile(f"diff{t}", tag)
+            subtract(t, whole)
+
+        difference(0)
+        nc.vector.tensor_copy(
+            w_bf[:].rearrange("p (t g u j) -> p t g u j", t=SLOTS, u=RUN, j=SLOTS),
+            w_raw[:].rearrange("p j (g t u) -> p t g u j", t=SLOTS, u=RUN),
+        )
+        difference(1)
+        difference(2, "b_xb")
+        gated(0, whole)
+        gated(1, whole)
+        nc.vector.quantize_mx(out=w_codes[:].bitcast(FP8X4), scales=w_plane[:], in_=w_bf[:])
+        nc.scalar.copy(wins[last][:, :S], b_banks[last][:])
+        fetch(first[last], last, n1_t, halves[0])
+        fetch(second[last], last, n2_t, halves[0])
+        diff[last] = rows_tile(f"diff{last}", "w_bf")
+        subtract(last, halves[0])
+        gated(2, whole)
+        fetch(first[last], last, n1_t, halves[1])
+        gated(last, halves[0])
+        fetch(second[last], last, n2_t, halves[1])
+
+        def dense_half(half, banks):
+            cols = halves[half]
+            z_bf = sb.tile([P, HALF * SLOTS], BF16, name=f"z_bf{half}", align_bytes=64)
+            z_codes = sb.tile([P, HALF], U32, name=f"z_codes{half}", align_bytes=64)
+            z_plane = sb.tile([P, HALF], U8, name=f"z_plane{half}", align_bytes=64)
+            nc.vector.tensor_copy(
+                z_bf[:].rearrange("p (j t) -> p j t", t=SLOTS), z_rows[:, :, cols].rearrange("p t j -> p j t")
+            )
+            nc.vector.quantize_mx(out=z_codes[:].bitcast(FP8X4), scales=z_plane[:], in_=z_bf[:])
+            for t in range(SLOTS):
+                product(banks[t], t, w_codes, w_plane, z_codes[:], z_plane[:])
+
+        subtract(last, halves[1])
+        early = ps.tile([P, SLOTS, HALF], F32, name="early")
+        dense_half(0, [early[:, t, :] for t in range(SLOTS)])
+        gated(last, halves[1])
+        late = [ps.tile([P, HALF], F32, name=f"bh{t}") for t in range(SLOTS)]
+        dense_half(1, [bank[:] for bank in late])
+        for t in range(SLOTS):
+            nc.scalar.copy(wins[t][:, halves[0]], early[:, t, :])
+        nc.scalar.copy(wins[0][:, halves[1]], late[0][:])
+        for t in range(1, SLOTS):
+            nc.vector.tensor_copy(wins[t][:, halves[1]], late[t][:])
+
+        out_rows = out.rearrange("(g t u) j -> t g u j", t=SLOTS, u=RUN)
+        for t in range(SLOTS):
+            g5, g6, g3, g4 = (rows_tile(f"g{n}_{t}") for n in (5, 6, 3, 4))
+            minus, plus, res = rows_tile(f"minus{t}"), rows_tile(f"plus{t}"), rows_tile(f"res{t}")
+            fetch(g5, t, n5_t, whole)
+            fetch(g6, t, n6_t, whole)
+            nc.vector.scalar_tensor_tensor(minus[:], g5[:], 0.75, g6[:], ALU.mult, ALU.mult)
+            fetch(g3, t, n3_t, whole)
+            for cols in halves if t == last else [whole]:
+                fetch(g4, t, n4_t, cols)
+                nc.vector.scalar_tensor_tensor(plus[:, cols], g3[:, cols], 0.75, g4[:, cols], ALU.mult, ALU.mult)
+                nc.vector.tensor_tensor(res[:, cols], plus[:, cols], minus[:, cols], ALU.subtract)
+                nc.sync.dma_start(out_rows[t][:, :, cols], res[:, cols])

@@ -62,10 +62,6 @@ def tile_picked_twpqjointbdet_none_p_kernel(
         n3_t = load_list("n3_t", n3)
         n4_t = load_list("n4_t", n4)
 
-        planes = {}
-        for name in ("b", "a"):
-            planes[name] = sb.tile([P, H + S], U8, name=name + "_plane", align_bytes=64)
-            nc.gpsimd.memset(planes[name][:].bitcast(I32), 0)
         wins = [sb.tile([P, WINDOW], F32, name=f"win{t}", align_bytes=64) for t in range(SLOTS)]
         for t in range(SLOTS):
             nc.gpsimd.memset(wins[t][:, S:], 0.0)
@@ -103,13 +99,14 @@ def tile_picked_twpqjointbdet_none_p_kernel(
 
         def scale_plane(name, dict_list, token_list, queue, tag):
             got = sb.tile([P, H + S], U8, name=name + "_bytes", tag=tag, align_bytes=64)
-            stage = sb.tile([P, H + S], U8, name=name + "_stage", align_bytes=64)
+            plane = sb.tile([P, H + S], U8, name=name + "_plane", align_bytes=64)
             nc.vector.tensor_copy(got[:, :H], ds_win[:].indirect(dict_list[:]))
             nc.vector.tensor_copy(got[:, H:], xs_win[:].indirect(token_list[:]))
-            deal(stage[:, :H].bitcast(I32), got[:, :H].bitcast(I32), RUN // 4)
-            nc.vector.tensor_copy(stage[:, H:].bitcast(I32), got[:, H:].bitcast(I32))
-            for r in range(4):
-                queue.dma_start(planes[name][r:P:32, :].bitcast(I32), stage[RUN * r : P : 32, :].bitcast(I32))
+            deal(plane[:, :H].bitcast(I32), got[:, :H].bitcast(I32), RUN // 4)
+            nc.vector.tensor_copy(plane[:, H:].bitcast(I32), got[:, H:].bitcast(I32))
+            for r in range(1, 4):
+                queue.dma_start(plane[r:P:32, :].bitcast(I32), plane[RUN * r : P : 32, :].bitcast(I32))
+            return plane
 
         def dict_words(name, dict_list, tag):
             d_got = sb.tile([P, H], U32, name=name + "_dg", tag=tag, align_bytes=64)
@@ -121,26 +118,23 @@ def tile_picked_twpqjointbdet_none_p_kernel(
             deal(d_codes[:].bitcast(I32), d_got[:].bitcast(I32), RUN)
             return d_codes
 
-        scale_plane("b", k2_t, two_t, nc.scalar, "b_xb")
+        b_plane = scale_plane("b", k2_t, two_t, nc.scalar, "b_xb")
         b_got = dict_words("b", k2_t, "b_dg")
         b_x = token_words("b", two_t)
         b_d = dealt_words("b", b_got)
         a_x = token_words("a", offs_t)
         b_banks = [ps.tile([P, S], F32, name=f"bh{t}") for t in range(SLOTS)]
         for t in range(SLOTS):
-            product(b_banks[t][:], t, b_d, planes["b"], b_x[:], planes["b"][:, H:])
+            product(b_banks[t][:], t, b_d, b_plane, b_x[:], b_plane[:, H:])
 
-        w_raw = sb.tile([P, SLOTS, N], F32, name="w_raw", tag="b_xb", align_bytes=64)
+        w_raw = sb.tile([P, SLOTS, N], F32, name="w_raw", tag="b_dg", align_bytes=64)
         w_rows = w1.rearrange("(g t u) m -> t g u m", t=SLOTS, u=RUN)
         for t in range(SLOTS):
             nc.sync.dma_start(w_raw[:, t, :], w_rows[t])
 
-        scale_plane("a", k1_t, offs_t, nc.sync, "xw_win")
-        a_d = dealt_words("a", dict_words("a", k1_t, "b_xc"))
+        a_plane = scale_plane("a", k1_t, offs_t, nc.sync, "xw_win")
         a_pairs = [ps.tile([P, 2, S], F32, name=f"a{pair}") for pair in range(2)]
         a_rows = [a_pairs[t // 2][:, t % 2, :] for t in range(SLOTS)]
-        for t in range(SLOTS):
-            product(a_rows[t], t, a_d, planes["a"], a_x[:], planes["a"][:, H:])
 
         def fetch(dst, t, lst, cols):
             nc.scalar.activation(dst[:, cols], wins[t][:].indirect(lst[:, cols.start // 16 : cols.stop // 16]), ACT.Copy)
@@ -152,74 +146,93 @@ def tile_picked_twpqjointbdet_none_p_kernel(
         halves = [slice(0, HALF), slice(HALF, S)]
         last = SLOTS - 1
 
-        w_bf = sb.tile([P, N * SLOTS], BF16, name="w_bf", align_bytes=64)
         w_codes = sb.tile([P, N], U32, name="w_codes", align_bytes=64)
         w_plane = sb.tile([P, N], U8, name="w_plane", align_bytes=64)
         z_rows = sb.tile([P, SLOTS, S], BF16, name="z_rows", align_bytes=64)
+        z_codes = [sb.tile([P, HALF], U32, name=f"z_codes{half}", align_bytes=64) for half in range(2)]
+        z_plane = [sb.tile([P, HALF], U8, name=f"z_plane{half}", align_bytes=64) for half in range(2)]
         first = [rows_tile(f"first{t}") for t in range(SLOTS)]
         second = [rows_tile(f"second{t}") for t in range(SLOTS)]
-        diff = {}
         gate = [rows_tile(f"gate{t}") for t in range(SLOTS)]
+        diff = [rows_tile(f"diff{t}") for t in range(SLOTS)]
+
+        def weight_tile(t, tag):
+            w_bf = sb.tile([P, P * SLOTS], BF16, name=f"w_bf{t}", tag=tag, align_bytes=64)
+            nc.vector.tensor_copy(
+                w_bf[:].rearrange("p (g c i j) -> p g c j i", c=2, i=4, j=SLOTS),
+                w_raw[:].rearrange("p j (g t c i) -> p t g c j i", t=SLOTS, c=2, i=4)[:, t],
+            )
+            cols = slice(t * P, (t + 1) * P)
+            nc.vector.quantize_mx(out=w_codes[:, cols].bitcast(FP8X4), scales=w_plane[:, cols], in_=w_bf[:])
 
         def subtract(t, cols):
             nc.vector.tensor_tensor(diff[t][:, cols], first[t][:, cols], second[t][:, cols], ALU.subtract)
 
-        def gated(t, cols):
+        def squash(t, cols):
             nc.scalar.activation(gate[t][:, cols], diff[t][:, cols], ACT.Tanh, scale=0.0625)
+
+        def gated(t, cols):
             nc.vector.scalar_tensor_tensor(
                 z_rows[:, t, cols], a_rows[t][:, cols], gn16[:, t : t + 1], gate[t][:, cols], ALU.mult, ALU.mult
             )
 
-        def difference(t, tag=None):
-            nc.scalar.copy(wins[t][:, :S], b_banks[t][:])
+        z_bf = [sb.tile([P, HALF * SLOTS], BF16, name=f"z_bf{half}", align_bytes=64) for half in range(2)]
+
+        def interleave(half):
+            nc.vector.tensor_copy(
+                z_bf[half][:].rearrange("p (c i t) -> p c t i", i=4, t=SLOTS),
+                z_rows[:, :, halves[half]].rearrange("p t (c i) -> p c t i", i=4),
+            )
+
+        def quantise(half):
+            nc.vector.quantize_mx(out=z_codes[half][:].bitcast(FP8X4), scales=z_plane[half][:], in_=z_bf[half][:])
+
+        def difference(t):
             fetch(first[t], t, n1_t, whole)
             fetch(second[t], t, n2_t, whole)
-            diff[t] = rows_tile(f"diff{t}", tag)
             subtract(t, whole)
 
+        for t in range(2):
+            nc.scalar.copy(wins[t][:, :S], b_banks[t][:])
+        for t in range(2, SLOTS):
+            nc.vector.tensor_copy(wins[t][:, :S], b_banks[t][:])
         difference(0)
-        nc.vector.tensor_copy(
-            w_bf[:].rearrange("p (t g u j) -> p t g u j", t=SLOTS, u=RUN, j=SLOTS),
-            w_raw[:].rearrange("p j (g t u) -> p t g u j", t=SLOTS, u=RUN),
-        )
+        a_d = dealt_words("a", dict_words("a", k1_t, "first0"))
+        for t in range(SLOTS):
+            product(a_rows[t], t, a_d, a_plane, a_x[:], a_plane[:, H:])
         difference(1)
-        difference(2, "b_xb")
+        squash(0, whole)
+        weight_tile(0, "w_bf0")
         gated(0, whole)
+        difference(2)
+        squash(1, whole)
         gated(1, whole)
-        nc.vector.quantize_mx(out=w_codes[:].bitcast(FP8X4), scales=w_plane[:], in_=w_bf[:])
-        nc.scalar.copy(wins[last][:, :S], b_banks[last][:])
         fetch(first[last], last, n1_t, halves[0])
         fetch(second[last], last, n2_t, halves[0])
-        diff[last] = rows_tile(f"diff{last}", "w_bf")
         subtract(last, halves[0])
+        squash(2, whole)
         gated(2, whole)
         fetch(first[last], last, n1_t, halves[1])
+        squash(last, halves[0])
         gated(last, halves[0])
         fetch(second[last], last, n2_t, halves[1])
-
-        def dense_half(half, banks):
-            cols = halves[half]
-            z_bf = sb.tile([P, HALF * SLOTS], BF16, name=f"z_bf{half}", align_bytes=64)
-            z_codes = sb.tile([P, HALF], U32, name=f"z_codes{half}", align_bytes=64)
-            z_plane = sb.tile([P, HALF], U8, name=f"z_plane{half}", align_bytes=64)
-            nc.vector.tensor_copy(
-                z_bf[:].rearrange("p (j t) -> p j t", t=SLOTS), z_rows[:, :, cols].rearrange("p t j -> p j t")
-            )
-            nc.vector.quantize_mx(out=z_codes[:].bitcast(FP8X4), scales=z_plane[:], in_=z_bf[:])
-            for t in range(SLOTS):
-                product(banks[t], t, w_codes, w_plane, z_codes[:], z_plane[:])
-
         subtract(last, halves[1])
-        early = ps.tile([P, SLOTS, HALF], F32, name="early")
-        dense_half(0, [early[:, t, :] for t in range(SLOTS)])
+        interleave(0)
+        squash(last, halves[1])
         gated(last, halves[1])
-        late = [ps.tile([P, HALF], F32, name=f"bh{t}") for t in range(SLOTS)]
-        dense_half(1, [bank[:] for bank in late])
-        for t in range(SLOTS):
-            nc.scalar.copy(wins[t][:, halves[0]], early[:, t, :])
-        nc.scalar.copy(wins[0][:, halves[1]], late[0][:])
+        quantise(0)
+        interleave(1)
+        quantise(1)
+        for half, cols in enumerate(halves):
+            bank = ps.tile([P, HALF], F32, name=f"half{half}")
+            product(bank[:], 0, w_codes, w_plane, z_codes[half][:], z_plane[half][:])
+            nc.scalar.copy(wins[0][:, cols], bank[:])
         for t in range(1, SLOTS):
-            nc.vector.tensor_copy(wins[t][:, halves[1]], late[t][:])
+            weight_tile(t, "z_bf1")
+            bank = ps.tile([P, S], F32, name=f"bh{t}")
+            for half, cols in enumerate(halves):
+                product(bank[:, cols], t, w_codes, w_plane, z_codes[half][:], z_plane[half][:])
+            nc.vector.tensor_copy(wins[t][:, :S], bank[:])
 
         out_rows = out.rearrange("(g t u) j -> t g u j", t=SLOTS, u=RUN)
         for t in range(SLOTS):

from contextlib import ExitStack

import concourse.mybir as mybir

K, T, S, N, G, H = 512, 1024, 256, 512, 2048, 512
FLOPS = 3 * 2 * 512 * 512 * 256

F32 = mybir.dt.float32
BF16 = mybir.dt.bfloat16
I32 = mybir.dt.int32
U32 = mybir.dt.uint32
U16 = mybir.dt.uint16
U8 = mybir.dt.uint8
FP8X4 = mybir.dt.float8_e4m3fn_x4
ACT = mybir.ActivationFunctionType
ALU = mybir.AluOpType

P = 128
SLOTS = 4
RUN = 8
WINDOW = 2 * S
HALF = S // 2


def tile_picked_twpqjointbdet_none_p_kernel(
    tc, x_words, x_scales, d_words, d_scales, gn, w1, offs, k1, two, k2, n1, n2, n3, n4, n5, n6, out
):
    nc = tc.nc
    with ExitStack() as ctx:
        sb = ctx.enter_context(tc.tile_pool(name="sb", bufs=1))
        ps = ctx.enter_context(tc.psum_pool(name="ps", bufs=1))

        def load_list(name, src):
            tile = sb.tile([P, src.shape[1]], U16, name=name)
            nc.sync.dma_start(tile[:], src)
            return tile

        def load_scales(name, src):
            width = src.shape[2]
            tile = sb.tile([P, width], U8, name=name, align_bytes=64)
            rows = src[0].bitcast(I32).unsqueeze(1).to_broadcast([16, RUN, width // 4])
            nc.scalar.dma_start(tile[:].bitcast(I32), rows)
            return tile

        def load_words(name, src, queue):
            tile = sb.tile([P, src.shape[2]], I32, name=name, align_bytes=64)
            queue.dma_start(tile[:], src[0].rearrange("p n t -> p (n t)").bitcast(I32))
            return tile

        ds_win = load_scales("ds_win", d_scales)
        k2_t = load_list("k2_t", k2)
        xs_win = load_scales("xs_win", x_scales)
        two_t = load_list("two_t", two)
        dw_win = load_words("dw_win", d_words, nc.scalar)
        k1_t = load_list("k1_t", k1)
        offs_t = load_list("offs_t", offs)
        n1_t = load_list("n1_t", n1)
        n2_t = load_list("n2_t", n2)
        n5_t = load_list("n5_t", n5)
        xw_win = load_words("xw_win", x_words, nc.sync)
        n6_t = load_list("n6_t", n6)
        n3_t = load_list("n3_t", n3)
        n4_t = load_list("n4_t", n4)

        wins = [sb.tile([P, WINDOW], F32, name=f"win{t}", align_bytes=64) for t in range(SLOTS)]
        for t in range(SLOTS):
            nc.gpsimd.memset(wins[t][:, S:], 0.0)

        gn_raw = sb.tile([P, 8 * SLOTS], F32, name="gn_raw")
        gn_rows = gn.rearrange("(g t u) o -> t g u o", t=SLOTS, u=RUN)
        with nc.allow_non_contiguous_dma(reason="one gain for each partition and slot"):
            for t in range(SLOTS):
                nc.gpsimd.dma_start(gn_raw[:, 8 * t : 8 * t + 1], gn_rows[t])
        gn16 = sb.tile([P, SLOTS], F32, name="gn16")
        nc.gpsimd.tensor_scalar(gn16[:], gn_raw[:, ::8], 0.0625, 0.0, ALU.mult, ALU.add)

        def deal(dst, src, run):
            nc.vector.tensor_copy(
                dst.rearrange("p (t g u) -> p t g u", t=SLOTS, u=run),
                src.rearrange("p (g t u) -> p t g u", t=SLOTS, u=run),
            )

        def product(bank, t, lhs, lhs_scale, rhs, rhs_scale):
            cols = slice(t * P, (t + 1) * P)
            nc.tensor.matmul_mx(
                out=bank,
                lhsT=lhs[:, cols].bitcast(FP8X4),
                lhsT_scale=lhs_scale[:, cols],
                rhs=rhs.bitcast(FP8X4),
                rhs_scale=rhs_scale,
                start=True,
                stop=True,
            )

        def token_words(name, token_list):
            x_codes = sb.tile([P, S], U32, name=name + "_xc", align_bytes=64)
            nc.vector.tensor_copy(x_codes[:], xw_win[:].bitcast(U32).indirect(token_list[:]))
            return x_codes

        def scale_plane(name, dict_list, token_list, queue, tag):
            got = sb.tile([P, H + S], U8, name=name + "_bytes", tag=tag, align_bytes=64)
            plane = sb.tile([P, H + S], U8, name=name + "_plane", align_bytes=64)
            nc.vector.tensor_copy(got[:, :H], ds_win[:].indirect(dict_list[:]))
            nc.vector.tensor_copy(got[:, H:], xs_win[:].indirect(token_list[:]))
            deal(plane[:, :H].bitcast(I32), got[:, :H].bitcast(I32), RUN // 4)
            nc.vector.tensor_copy(plane[:, H:].bitcast(I32), got[:, H:].bitcast(I32))
            for r in range(1, 4):
                queue.dma_start(plane[r:P:32, :].bitcast(I32), plane[RUN * r : P : 32, :].bitcast(I32))
            return plane

        def dict_words(name, dict_list, tag):
            d_got = sb.tile([P, H], U32, name=name + "_dg", tag=tag, align_bytes=64)
            nc.vector.tensor_copy(d_got[:], dw_win[:].bitcast(U32).indirect(dict_list[:]))
            return d_got

        def dealt_words(name, d_got):
            d_codes = sb.tile([P, H], U32, name=name + "_dc", align_bytes=64)
            deal(d_codes[:].bitcast(I32), d_got[:].bitcast(I32), RUN)
            return d_codes

        b_plane = scale_plane("b", k2_t, two_t, nc.scalar, "b_xb")
        b_got = dict_words("b", k2_t, "b_dg")
        b_x = token_words("b", two_t)
        b_d = dealt_words("b", b_got)
        a_x = token_words("a", offs_t)
        b_banks = [ps.tile([P, S], F32, name=f"bh{t}") for t in range(SLOTS)]
        for t in range(SLOTS):
            product(b_banks[t][:], t, b_d, b_plane, b_x[:], b_plane[:, H:])

        w_raw = sb.tile([P, SLOTS, N], F32, name="w_raw", tag="b_dg", align_bytes=64)
        w_rows = w1.rearrange("(g t u) m -> t g u m", t=SLOTS, u=RUN)
        for t in range(SLOTS):
            nc.sync.dma_start(w_raw[:, t, :], w_rows[t])

        a_plane = scale_plane("a", k1_t, offs_t, nc.sync, "xw_win")
        a_pairs = [ps.tile([P, 2, S], F32, name=f"a{pair}") for pair in range(2)]
        a_rows = [a_pairs[t // 2][:, t % 2, :] for t in range(SLOTS)]

        def fetch(dst, t, lst, cols):
            nc.scalar.activation(dst[:, cols], wins[t][:].indirect(lst[:, cols.start // 16 : cols.stop // 16]), ACT.Copy)

        def rows_tile(name, tag=None):
            return sb.tile([P, S], F32, name=name, tag=tag or name, align_bytes=64)

        whole = slice(0, S)
        halves = [slice(0, HALF), slice(HALF, S)]
        last = SLOTS - 1

        w_codes = sb.tile([P, N], U32, name="w_codes", align_bytes=64)
        w_plane = sb.tile([P, N], U8, name="w_plane", align_bytes=64)
        z_rows = sb.tile([P, SLOTS, S], BF16, name="z_rows", align_bytes=64)
        z_codes = [sb.tile([P, HALF], U32, name=f"z_codes{half}", align_bytes=64) for half in range(2)]
        z_plane = [sb.tile([P, HALF], U8, name=f"z_plane{half}", align_bytes=64) for half in range(2)]
        first = [rows_tile(f"first{t}") for t in range(SLOTS)]
        second = [rows_tile(f"second{t}") for t in range(SLOTS)]
        gate = [rows_tile(f"gate{t}") for t in range(SLOTS)]
        diff = [rows_tile(f"diff{t}") for t in range(SLOTS)]

        def weight_tile(t, tag):
            w_bf = sb.tile([P, P * SLOTS], BF16, name=f"w_bf{t}", tag=tag, align_bytes=64)
            nc.vector.tensor_copy(
                w_bf[:].rearrange("p (g c i j) -> p g c j i", c=2, i=4, j=SLOTS),
                w_raw[:].rearrange("p j (g t c i) -> p t g c j i", t=SLOTS, c=2, i=4)[:, t],
            )
            cols = slice(t * P, (t + 1) * P)
            nc.vector.quantize_mx(out=w_codes[:, cols].bitcast(FP8X4), scales=w_plane[:, cols], in_=w_bf[:])

        def subtract(t, cols):
            nc.vector.tensor_tensor(diff[t][:, cols], first[t][:, cols], second[t][:, cols], ALU.subtract)

        def squash(t, cols):
            nc.scalar.activation(gate[t][:, cols], diff[t][:, cols], ACT.Tanh, scale=0.0625)

        def gated(t, cols):
            nc.vector.scalar_tensor_tensor(
                z_rows[:, t, cols], a_rows[t][:, cols], gn16[:, t : t + 1], gate[t][:, cols], ALU.mult, ALU.mult
            )

        z_bf = [sb.tile([P, HALF * SLOTS], BF16, name=f"z_bf{half}", align_bytes=64) for half in range(2)]

        def interleave(half):
            nc.vector.tensor_copy(
                z_bf[half][:].rearrange("p (c i t) -> p c t i", i=4, t=SLOTS),
                z_rows[:, :, halves[half]].rearrange("p t (c i) -> p c t i", i=4),
            )

        def quantise(half):
            nc.vector.quantize_mx(out=z_codes[half][:].bitcast(FP8X4), scales=z_plane[half][:], in_=z_bf[half][:])

        def difference(t):
            fetch(first[t], t, n1_t, whole)
            fetch(second[t], t, n2_t, whole)
            subtract(t, whole)

        for t in range(2):
            nc.scalar.copy(wins[t][:, :S], b_banks[t][:])
        for t in range(2, SLOTS):
            nc.vector.tensor_copy(wins[t][:, :S], b_banks[t][:])
        difference(0)
        a_d = dealt_words("a", dict_words("a", k1_t, "first0"))
        for t in range(SLOTS):
            product(a_rows[t], t, a_d, a_plane, a_x[:], a_plane[:, H:])
        difference(1)
        squash(0, whole)
        weight_tile(0, "w_bf0")
        gated(0, whole)
        difference(2)
        squash(1, whole)
        gated(1, whole)
        fetch(first[last], last, n1_t, halves[0])
        fetch(second[last], last, n2_t, halves[0])
        subtract(last, halves[0])
        squash(2, whole)
        gated(2, whole)
        fetch(first[last], last, n1_t, halves[1])
        squash(last, halves[0])
        gated(last, halves[0])
        fetch(second[last], last, n2_t, halves[1])
        subtract(last, halves[1])
        interleave(0)
        squash(last, halves[1])
        gated(last, halves[1])
        quantise(0)
        interleave(1)
        quantise(1)
        for half, cols in enumerate(halves):
            bank = ps.tile([P, HALF], F32, name=f"half{half}")
            product(bank[:], 0, w_codes, w_plane, z_codes[half][:], z_plane[half][:])
            nc.scalar.copy(wins[0][:, cols], bank[:])
        for t in range(1, SLOTS):
            weight_tile(t, "z_bf1")
            bank = ps.tile([P, S], F32, name=f"bh{t}")
            for half, cols in enumerate(halves):
                product(bank[:, cols], t, w_codes, w_plane, z_codes[half][:], z_plane[half][:])
            nc.vector.tensor_copy(wins[t][:, :S], bank[:])

        out_rows = out.rearrange("(g t u) j -> t g u j", t=SLOTS, u=RUN)
        for t in range(SLOTS):
            g5, g6, g3, g4 = (rows_tile(f"g{n}_{t}") for n in (5, 6, 3, 4))
            minus, plus, res = rows_tile(f"minus{t}"), rows_tile(f"plus{t}"), rows_tile(f"res{t}")
            fetch(g5, t, n5_t, whole)
            fetch(g6, t, n6_t, whole)
            nc.vector.scalar_tensor_tensor(minus[:], g5[:], 0.75, g6[:], ALU.mult, ALU.mult)
            fetch(g3, t, n3_t, whole)
            for cols in halves if t == last else [whole]:
                fetch(g4, t, n4_t, cols)
                nc.vector.scalar_tensor_tensor(plus[:, cols], g3[:, cols], 0.75, g4[:, cols], ALU.mult, ALU.mult)
                nc.vector.tensor_tensor(res[:, cols], plus[:, cols], minus[:, cols], ALU.subtract)
                nc.sync.dma_start(out_rows[t][:, :, cols], res[:, cols])
